import numpy as np, ml_dtypes
CORES = [51,54,179,182]
N = 4
import mx_ref
NC, G = 512, 2
C, C2 = np.float32(0.031), np.float32(0.023)
CNT = [[48,352,0,112],[0,0,192,320],[112,160,160,80],[352,0,160,0]]
OFF = [[sum(c[:e]) for e in range(N + 1)] for c in CNT]
BF = ml_dtypes.bfloat16
def cut(t, i, w=512):
    return t[:, w * i:w * i + w]
def tile(rs):
    return np.stack(rs, axis=2).reshape(128, -1).astype(BF)
def layer(w, X):
    out = []
    for i in range(G):
        for t in range(len(X)):
            p = mx_ref.matmul(mx_ref.quantize(cut(w, len(X) * i + t)), X[t])
            z = p if t == 0 else z + p
        out.append(z)
    return out
def act(Z):
    return [np.maximum(s * z, 0) * C for z in Z for s in (1, -1)]
def setup_inputs(rng):
    def f(*shape):
        return mx_ref.flush((rng.standard_normal(shape, dtype=np.float32) * np.exp2(rng.integers(-2, 3, shape[:-1] + (1,)))).astype(BF))
    return {"x": f(N, 128, 4 * NC), "w1": f(N, 128, G * 512), "w2": f(N, 128, G * 512), "w3": f(N, 128, 512)}
def setup_inputs_blocks(rng):
    d = setup_inputs(rng)
    for k in ("x", "w3"): d[k] = mx_ref.spread(d[k], rng, 4)
    for k in ("w1", "w2"): d[k] = mx_ref.spread(d[k], rng, 2)
    return d
def setup_inputs_wide(rng):
    d = setup_inputs(rng)
    for k in ("x", "w1", "w2", "w3"): d[k] = mx_ref.flush((d[k].astype(np.float32) * np.exp2(rng.integers(-4, 5, (N, 1, 1))).astype(np.float32)).astype(BF))
    return d
def setup_inputs_zeros(rng):
    d = setup_inputs(rng); v = d["x"].reshape(N, 128, -1, 4).copy()
    v[np.broadcast_to((rng.random((N, 1, v.shape[2], 1)) < 0.33), v.shape)] = 0
    d["x"] = v.reshape(d["x"].shape)
    return d
def act2(Z):
    return [np.maximum(s * z, 0) * C2 for z in Z for s in (1, -1)]
def reference(x, w1, w2, w3):
    h = [tile(act(layer(w1[j], [mx_ref.quantize(x[j])]))) for j in range(N)]
    g = []
    for e in range(N):
        t = np.concatenate([h[j][:, 4 * OFF[j][e]:4 * OFF[j][e + 1]] for j in range(N)], axis=1)
        g.append(tile(act2(layer(w2[e], [mx_ref.quantize(t)]))))
    y = np.zeros((N, 128, NC), np.float32)
    for j in range(N):
        back = []
        for e in range(N):
            a = sum(CNT[i][e] for i in range(j))
            back.append(g[e][:, 4 * a:4 * a + 4 * CNT[j][e]])
        y[j] = mx_ref.matmul(mx_ref.quantize(w3[j]), mx_ref.quantize(np.concatenate(back, axis=1)))
    return {"y": y}

@@ -1,0 +1,264 @@
+import numpy as np
+from concourse.bass import DstId, RemoteDMATransfer
+from concourse.mybir import dt, AluOpType, ActivationFunctionType
+
+NC = 512
+MIN = 128
+WC = 256
+RANKS = 4
+CUT = 256
+C1, C2 = float(np.float32(0.031)), float(np.float32(0.023))
+XCH = [(0, 256), (256, 512)]
+MAXSTEP = 6
+
+SCRATCH = {
+    "xt": ("sbuf", [128, 4 * NC], "bfloat16"), "w1t": ("sbuf", [128, 1024], "bfloat16"),
+    "w2t": ("sbuf", [128, 1024], "bfloat16"), "w3t": ("sbuf", [128, 512], "bfloat16"),
+    "ht": ("sbuf", [128, 4 * NC], "bfloat16"), "gt": ("sbuf", [128, 4 * NC], "bfloat16"),
+    "ysb": ("sbuf", [128, NC], "float32"),
+    "ps": ("psum", [128, 512 * 8], "float32"),
+}
+for _n, _w in [("x", NC), ("w1", WC), ("w2", WC), ("w3", 128), ("h", NC), ("g", NC)] + [("r%d" % _e, WC) for _e in range(RANKS)]:
+    SCRATCH["q" + _n] = ("sbuf", [128, _w], "float8_e4m3fn_x4")
+    SCRATCH["s" + _n] = ("sbuf", [128, _w], "uint8")
+
+SEMAPHORES = ["lw1", "lw2a", "lw2b", "lw3", "qw1", "qw2", "qw3", "sent"]
+SEMAPHORES += ["%s%d" % (n, c) for c in range(len(XCH)) for n in ("lx", "qx", "ha", "qh", "za", "zb")]
+SEMAPHORES += ["arr%d" % e for e in range(RANKS)]
+SEMAPHORES += ["%s%d" % (n, s) for s in range(MAXSTEP) for n in ("ya", "yb", "ga", "qg", "yo", "yc", "st")]
+
+
+def sends(cnt, cores, rank, topo):
+    def here(d):
+        return topo.host(cores[d]) == topo.host(cores[rank]) and topo.chip(cores[d]) == topo.chip(cores[rank])
+    need = sorted((d for d in range(len(cores)) if d != rank and cnt[d][rank]), key=lambda d: -cnt[d][rank])
+    return [d for d in need if here(d)], [d for d in need if not here(d)]
+
+
+def plan(cnt, cores, rank, topo):
+    off = [sum(cnt[rank][:e]) for e in range(len(cores) + 1)]
+    segs = []
+    for e in range(len(cores)):
+        if not cnt[rank][e]:
+            continue
+        if e == rank:
+            key = 0
+        else:
+            on, out = sends(cnt, cores, e, topo)
+            key = 1 if rank in on else 2 + out.index(rank)
+        segs.append((key, e, off[e], off[e + 1]))
+    steps = []
+    for key, e, a, b in sorted(segs):
+        m = a + (b - a) // 4 * 2 if b - a > CUT else b
+        for p, q in [(a, m), (m, b)]:
+            if q > p:
+                steps.append((e, p, q, key > 2))
+    state = [0] * NC
+    units = []
+    for _, a, b, _l in steps:
+        state[a:b] = [1] * (b - a)
+        got = []
+        while True:
+            found = None
+            i = 0
+            while i < NC:
+                j = i
+                while j < NC and state[j] == state[i]:
+                    j += 1
+                if state[i] == 1:
+                    lo, hi = i, j
+                    k = lo
+                    while k > 0 and state[k - 1] == 0:
+                        k -= 1
+                    if 0 < lo - k < MIN:
+                        lo += MIN - (lo - k)
+                    k = hi
+                    while k < NC and state[k] == 0:
+                        k += 1
+                    if 0 < k - hi < MIN:
+                        hi -= MIN - (k - hi)
+                    if hi - lo >= MIN:
+                        found = (lo, hi)
+                        break
+                i = j
+            if found is None:
+                break
+            state[found[0]:found[1]] = [2] * (found[1] - found[0])
+            got.append(found)
+        units.append(got)
+    return steps, units
+
+
+def rank_program(g, core, T, topo):
+    rank = T.rank_of(core)
+    if rank is None:
+        return
+    cnt, cores, S = T.tables["CNT"], T.cores, T.sem
+    steps, units = plan(cnt, cores, rank, topo)
+    act, vec, ten, sync = g.scalar, g.vector, g.tensor, g.sync
+    relu, copy = ActivationFunctionType.Relu, ActivationFunctionType.Copy
+
+    sync.dma_start(T.w2t[:, 0:512], T.w2[:, 0:512]).then_inc(S.lw2a, 16)
+    act.dma_start(T.w2t[:, 512:1024], T.w2[:, 512:1024]).then_inc(S.lw2b, 16)
+    sync.dma_start(T.w1t[:], T.w1[:]).then_inc(S.lw1, 16)
+    for c, (a, b) in enumerate(XCH):
+        q = act if c % 2 == 0 else sync
+        q.dma_start(T.xt[:, 4 * a:4 * b], T.x[:, 4 * a:4 * b]).then_inc(S["lx%d" % c], 16)
+    act.dma_start(T.w3t[:], T.w3[:]).then_inc(S.lw3, 16)
+
+    vec.wait_ge(S.lw2a, 16)
+    vec.quantize_mx(T.qw2[:, 0:128], T.sw2[:, 0:128], T.w2t[:, 0:512]).then_inc(S.qw2, 1)
+    vec.wait_ge(S.lw2b, 16)
+    vec.quantize_mx(T.qw2[:, 128:256], T.sw2[:, 128:256], T.w2t[:, 512:1024]).then_inc(S.qw2, 1)
+
+    on, out = sends(cnt, cores, rank, topo)
+    far = topo.mask(core, cores[out[0]])
+    arr = S["arr%d" % rank]
+    sent = [0]
+
+    def transfer(d, codes, mask):
+        rid, pid = topo.addr(cores[d], core)
+        if codes:
+            src, dst = T.qw2[:].bitcast(dt.uint8), T["qr%d" % rank][:].bitcast(dt.uint8)
+        else:
+            src, dst = T.sw2[:], T["sr%d" % rank][:]
+        sent[0] += mask.bit_count()
+        return RemoteDMATransfer(src=src, dst=dst, dst_ids=[DstId(rid=rid, pnc=pid)], dma_engine_mask=mask, remote_sem=arr)
+
+    g.wait_ge(S.qw2, 2)
+    for k, d in enumerate(out):
+        for codes in (True, False):
+            ts = [transfer(d, codes, far)]
+            if k == 0:
+                ts += [transfer(o, codes, topo.mask(core, cores[o]) & ~far) for o in on]
+            g.remote_dma_fused(ts, local_sem=S.sent)
+
+    vec.wait_ge(S.lw1, 16)
+    vec.quantize_mx(T.qw1[:], T.sw1[:], T.w1t[:]).then_inc(S.qw1, 1)
+    bank = [0]
+    free = {}
+    waited = {}
+
+    def twait(name, n):
+        if waited.get(name, 0) < n:
+            ten.wait_ge(S[name], n)
+            waited[name] = n
+
+    def take():
+        b = bank[0] % 8
+        bank[0] += 1
+        if b in free:
+            twait(*free[b])
+        return b
+
+    def pair(w, sw, q, s, a, b, done):
+        bs = []
+        for i in range(2):
+            k = take()
+            ten.matmul_mx(T.ps[:, 512 * k:512 * k + b - a], w[:, 128 * i:128 * i + 128], sw[:, 128 * i:128 * i + 128],
+                          q[:, a:b], s[:, a:b], True, True).then_inc(S[done[i]], 1)
+            bs.append(k)
+        return bs
+
+    def acts(t, bs, skip, a, b, c, done, ev):
+        for i, q in ((0, act), (1, vec)):
+            q.wait_ge(S[done[i]], 1)
+            src = T.ps[:, 512 * bs[i] + skip:512 * bs[i] + skip + b - a]
+            for n, sign in ((0, 1.0), (1, -1.0)):
+                dst = t[:, 4 * a + 2 * i + n:4 * b:4]
+                if i == 0:
+                    act.activation(dst, src, relu, scale=sign * c).then_inc(S[ev], 1)
+                else:
+                    vec.tensor_scalar(dst, src, sign * c, 0.0, AluOpType.mult, AluOpType.max).then_inc(S[ev], 1)
+
+    def quant_x(c):
+        a, b = XCH[c]
+        vec.wait_ge(S["lx%d" % c], 16)
+        vec.quantize_mx(T.qx[:, a:b], T.sx[:, a:b], T.xt[:, 4 * a:4 * b]).then_inc(S["qx%d" % c], 1)
+
+    quant_x(0)
+    for c, (a, b) in enumerate(XCH):
+        done = ("za%d" % c, "zb%d" % c)
+        twait("qw1", 1)
+        twait("qx%d" % c, 1)
+        bs = pair(T.qw1, T.sw1, T.qx, T.sx, a, b, done)
+        for k in bs:
+            free[k] = ("qh%d" % c, 1)
+        acts(T.ht, bs, 0, a, b, C1, done, "ha%d" % c)
+        if c + 1 < len(XCH):
+            quant_x(c + 1)
+        vec.wait_ge(S["ha%d" % c], 4)
+        vec.quantize_mx(T.qh[:, a:b], T.sh[:, a:b], T.ht[:, 4 * a:4 * b]).then_inc(S["qh%d" % c], 1)
+    vec.wait_ge(S.lw3, 16)
+    vec.quantize_mx(T.qw3[:], T.sw3[:], T.w3t[:]).then_inc(S.qw3, 1)
+
+    pending, leaving, nun = [], [], [0]
+
+    def product():
+        for u, a, b in pending:
+            twait("qw3", 1)
+            twait("qg%d" % u, 1)
+            k = take()
+            free[k] = ("yc%d" % u, 1)
+            ten.matmul_mx(T.ps[:, 512 * k:512 * k + b - a], T.qw3[:], T.sw3[:], T.qg[:, a:b], T.sg[:, a:b],
+                          True, True).then_inc(S["yo%d" % u], 1)
+            leaving.append((u, a, b, k))
+        pending.clear()
+
+    def leave():
+        for u, a, b, k in leaving:
+            src = T.ps[:, 512 * k:512 * k + b - a]
+            if u % 2 == 0:
+                act.wait_ge(S["yo%d" % u], 1)
+                act.activation(T.ysb[:, a:b], src, copy).then_inc(S["yc%d" % u], 1)
+            else:
+                vec.wait_ge(S["yo%d" % u], 1)
+                vec.tensor_copy(T.ysb[:, a:b], src).then_inc(S["yc%d" % u], 1)
+            sync.wait_ge(S["yc%d" % u], 1)
+            sync.dma_start(T.y[:, a:b], T.ysb[:, a:b]).then_inc(S["st%d" % u], 16)
+        leaving.clear()
+
+    seen = []
+    for s, (e, a, b, late) in enumerate(steps):
+        if late:
+            product()
+            leave()
+        lo, hi = a, b
+        if hi - lo < MIN:
+            lo = min(lo, NC - MIN)
+            hi = lo + MIN
+        for c, (p, q) in enumerate(XCH):
+            if p < hi and lo < q:
+                twait("qh%d" % c, 1)
+        if e == rank:
+            twait("qw2", 2)
+            w, sw = T.qw2, T.sw2
+        else:
+            son, sout = sends(cnt, cores, e, topo)
+            ofar = topo.mask(cores[e], cores[sout[0]])
+            m = ofar if rank in sout else topo.mask(cores[e], core) & ~ofar
+            twait("arr%d" % e, 2 * m.bit_count())
+            w, sw = T["qr%d" % e], T["sr%d" % e]
+        done, ev = ("ya%d" % s, "yb%d" % s), "ga%d" % s
+        bs = pair(w, sw, T.qh, T.sh, lo, hi, done)
+        for k in bs:
+            free[k] = (ev, 4)
+        product()
+        acts(T.gt, bs, a - lo, a, b, C2, done, ev)
+        seen.append((a, b, ev))
+        fresh = []
+        for p, q in units[s]:
+            for a2, b2, ev2 in seen:
+                if a2 < q and p < b2:
+                    vec.wait_ge(S[ev2], 4)
+            u = nun[0]
+            nun[0] += 1
+            vec.quantize_mx(T.qg[:, p:q], T.sg[:, p:q], T.gt[:, 4 * p:4 * q]).then_inc(S["qg%d" % u], 1)
+            fresh.append((u, p, q))
+        leave()
+        pending.extend(fresh)
+    product()
+    leave()
+    for u in range(nun[0]):
+        sync.wait_ge(S["st%d" % u], 16)
+    g.wait_ge(S.sent, sent[0])

@@ -8,31 +8,46 @@ WC = 256
 RANKS = 4
 CUT = 256
 C1, C2 = float(np.float32(0.031)), float(np.float32(0.023))
-XCH = [(0, 256), (256, 512)]
-MAXSTEP = 6
+BANKS = 8
+WAKE = 0.14
+SLACK = 0.04
+LOADED = {"w2a": 1.3, "w2b": 1.7, "w1": 2.8, "x0": 2.3, "x1": 3.7, "w3": 3.9}
+ARRIVE = [5.5, 5.5, 7.0]
+COST = {"quant": (0.03, 0.0009), "mm": (0.04, 0.0008), "S": (0.10, 0.00083), "V": (0.03, 0.00083), "store": (0.08, 0.0)}
 
 SCRATCH = {
     "xt": ("sbuf", [128, 4 * NC], "bfloat16"), "w1t": ("sbuf", [128, 1024], "bfloat16"),
     "w2t": ("sbuf", [128, 1024], "bfloat16"), "w3t": ("sbuf", [128, 512], "bfloat16"),
     "ht": ("sbuf", [128, 4 * NC], "bfloat16"), "gt": ("sbuf", [128, 4 * NC], "bfloat16"),
     "ysb": ("sbuf", [128, NC], "float32"),
-    "ps": ("psum", [128, 512 * 8], "float32"),
+    "ps": ("psum", [128, 512 * BANKS], "float32"),
 }
 for _n, _w in [("x", NC), ("w1", WC), ("w2", WC), ("w3", 128), ("h", NC), ("g", NC)] + [("r%d" % _e, WC) for _e in range(RANKS)]:
     SCRATCH["q" + _n] = ("sbuf", [128, _w], "float8_e4m3fn_x4")
     SCRATCH["s" + _n] = ("sbuf", [128, _w], "uint8")
 
-SEMAPHORES = ["lw1", "lw2a", "lw2b", "lw3", "qw1", "qw2", "qw3", "sent"]
-SEMAPHORES += ["%s%d" % (n, c) for c in range(len(XCH)) for n in ("lx", "qx", "ha", "qh", "za", "zb")]
-SEMAPHORES += ["arr%d" % e for e in range(RANKS)]
-SEMAPHORES += ["%s%d" % (n, s) for s in range(MAXSTEP) for n in ("ya", "yb", "ga", "qg", "yo", "yc", "st")]
+NTASK = 90
+SEMAPHORES = ["l" + n for n in LOADED] + ["%s%d" % (n, e) for e in range(RANKS) for n in ("codes", "plane")]
+SEMAPHORES += ["t%d" % i for i in range(NTASK)] + ["sent"]
+
+
+def here(a, b, topo):
+    return topo.host(a) == topo.host(b) and topo.chip(a) == topo.chip(b)
 
 
 def sends(cnt, cores, rank, topo):
-    def here(d):
-        return topo.host(cores[d]) == topo.host(cores[rank]) and topo.chip(cores[d]) == topo.chip(cores[rank])
     need = sorted((d for d in range(len(cores)) if d != rank and cnt[d][rank]), key=lambda d: -cnt[d][rank])
-    return [d for d in need if here(d)], [d for d in need if not here(d)]
+    return [d for d in need if here(cores[d], cores[rank], topo)], [d for d in need if not here(cores[d], cores[rank], topo)]
+
+
+def engines(cnt, cores, e, d, topo):
+    out = sends(cnt, cores, e, topo)[1]
+    far = topo.mask(cores[e], cores[out[0]])
+    if d == out[0]:
+        return far
+    if d in out:
+        return topo.mask(cores[out[0]], cores[d])
+    return topo.mask(cores[e], cores[d]) & ~far
 
 
 def plan(cnt, cores, rank, topo):
@@ -42,51 +57,104 @@ def plan(cnt, cores, rank, topo):
         if not cnt[rank][e]:
             continue
         if e == rank:
-            key = 0
+            key = -1
         else:
             on, out = sends(cnt, cores, e, topo)
-            key = 1 if rank in on else 2 + out.index(rank)
+            key = 0 if rank in on else 1 + out.index(rank)
         segs.append((key, e, off[e], off[e + 1]))
     steps = []
     for key, e, a, b in sorted(segs):
         m = a + (b - a) // 4 * 2 if b - a > CUT else b
         for p, q in [(a, m), (m, b)]:
             if q > p:
-                steps.append((e, p, q, key > 2))
+                steps.append((e, p, q, key))
     state = [0] * NC
     units = []
-    for _, a, b, _l in steps:
+    for _, a, b, _k in steps:
         state[a:b] = [1] * (b - a)
-        got = []
-        while True:
-            found = None
-            i = 0
-            while i < NC:
-                j = i
-                while j < NC and state[j] == state[i]:
-                    j += 1
-                if state[i] == 1:
-                    lo, hi = i, j
-                    k = lo
-                    while k > 0 and state[k - 1] == 0:
-                        k -= 1
-                    if 0 < lo - k < MIN:
-                        lo += MIN - (lo - k)
-                    k = hi
-                    while k < NC and state[k] == 0:
-                        k += 1
-                    if 0 < k - hi < MIN:
-                        hi -= MIN - (k - hi)
-                    if hi - lo >= MIN:
-                        found = (lo, hi)
-                        break
-                i = j
-            if found is None:
-                break
-            state[found[0]:found[1]] = [2] * (found[1] - found[0])
-            got.append(found)
-        units.append(got)
+        i = 0
+        while i < NC:
+            j = i
+            while j < NC and state[j] == state[i]:
+                j += 1
+            if state[i] == 1:
+                lo, hi, k = i, j, i
+                while k > 0 and state[k - 1] == 0:
+                    k -= 1
+                if 0 < lo - k < MIN:
+                    lo += MIN - (lo - k)
+                k = hi
+                while k < NC and state[k] == 0:
+                    k += 1
+                if 0 < k - hi < MIN:
+                    hi -= MIN - (k - hi)
+                if hi - lo >= MIN:
+                    state[lo:hi] = [2] * (hi - lo)
+                    units.append((lo, hi))
+            i = j
     return steps, units
+
+
+def halves(units):
+    lo, hi = units[0]
+    for a, b in units[1:]:
+        if hi - lo >= NC // 2 - 40 or (a != hi and b != lo):
+            break
+        lo, hi = min(lo, a), max(hi, b)
+    if lo == 0:
+        return [(0, hi), (hi, NC)]
+    return [(lo, NC), (0, lo)]
+
+
+def schedule(tasks):
+    users = [[] for _ in tasks]
+    for i, t in enumerate(tasks):
+        for d in t["deps"]:
+            users[d].append(i)
+
+    def dur(t, q):
+        c = COST[q] if t["kind"] == "act" else COST[t["kind"]]
+        return t["calls"] * (c[0] + c[1] * t["n"])
+    way = [0.0] * len(tasks)
+    for i in reversed(range(len(tasks))):
+        way[i] = max(dur(tasks[i], q) for q in tasks[i]["eng"]) + max([way[u] + WAKE for u in users[i]] + [0.0])
+    free = {}
+    banks = [(0.0, [])] * BANKS
+    holds = {}
+    order, left = [], set(range(len(tasks)))
+    while left:
+        cands = []
+        for i in sorted(left):
+            t = tasks[i]
+            if any(d in left for d in t["deps"]):
+                continue
+            at = max([t["at"]] + [tasks[d]["end"] + WAKE for d in t["deps"]])
+            bank = None
+            if t["kind"] == "mm":
+                ready = [(max(at, banks[k][0]), k) for k in range(BANKS) if banks[k] is not None]
+                if not ready:
+                    continue
+                at, bank = min(ready)
+            starts = [(max(at, free.get(q, 0.0)), q) for q in t["eng"]]
+            _, start, q = min((x + dur(t, q), x, q) for x, q in starts)
+            cands.append((start, -way[i], i, q, bank))
+        first = min(cands)
+        start, _, i, q, bank = min((c for c in cands if c[3] == first[3] and c[0] <= first[0] + SLACK), key=lambda c: c[1:4])
+        t = tasks[i]
+        left.remove(i)
+        order.append(i)
+        t["q"], t["start"], t["end"] = q, start, start + dur(t, q)
+        free[q] = t["end"]
+        if bank is not None:
+            t["deps"] = t["deps"] + banks[bank][1]
+            t["bank"] = bank
+            banks[bank] = None
+            holds[i] = bank
+        for d in t["deps"]:
+            if d in holds and t["kind"] == "act":
+                banks[holds[d]] = (t["end"] + WAKE, [i])
+                del holds[d]
+    return order
 
 
 def rank_program(g, core, T, topo):
@@ -95,170 +163,152 @@ def rank_program(g, core, T, topo):
         return
     cnt, cores, S = T.tables["CNT"], T.cores, T.sem
     steps, units = plan(cnt, cores, rank, topo)
-    act, vec, ten, sync = g.scalar, g.vector, g.tensor, g.sync
+    xch = halves(units)
+    queues = {"S": g.scalar, "V": g.vector, "T": g.tensor, "sync": g.sync}
     relu, copy = ActivationFunctionType.Relu, ActivationFunctionType.Copy
+    tasks = []
+    load = {}
+    come = {}
 
-    sync.dma_start(T.w2t[:, 0:512], T.w2[:, 0:512]).then_inc(S.lw2a, 16)
-    act.dma_start(T.w2t[:, 512:1024], T.w2[:, 512:1024]).then_inc(S.lw2b, 16)
-    sync.dma_start(T.w1t[:], T.w1[:]).then_inc(S.lw1, 16)
-    for c, (a, b) in enumerate(XCH):
-        q = act if c % 2 == 0 else sync
-        q.dma_start(T.xt[:, 4 * a:4 * b], T.x[:, 4 * a:4 * b]).then_inc(S["lx%d" % c], 16)
-    act.dma_start(T.w3t[:], T.w3[:]).then_inc(S.lw3, 16)
+    def task(kind, eng, n, deps, emit, calls=1, at=0.0):
+        tasks.append(dict(kind=kind, eng=eng, n=n, deps=deps, emit=emit, calls=calls, at=at))
+        return len(tasks) - 1
 
-    vec.wait_ge(S.lw2a, 16)
-    vec.quantize_mx(T.qw2[:, 0:128], T.sw2[:, 0:128], T.w2t[:, 0:512]).then_inc(S.qw2, 1)
-    vec.wait_ge(S.lw2b, 16)
-    vec.quantize_mx(T.qw2[:, 128:256], T.sw2[:, 128:256], T.w2t[:, 512:1024]).then_inc(S.qw2, 1)
+    def quant(q, s, t, a, b, deps, name=None):
+        i = task("quant", ["V"], b - a, deps,
+                 lambda v, me: v.quantize_mx(q[:, a:b], s[:, a:b], t[:, 4 * a:4 * b]), at=LOADED[name] + WAKE if name else 0.0)
+        if name:
+            load[i] = name
+        return i
 
-    on, out = sends(cnt, cores, rank, topo)
-    far = topo.mask(core, cores[out[0]])
-    arr = S["arr%d" % rank]
-    sent = [0]
+    def product(w, sw, k, q, s, a, b, deps, at=0.0):
+        return task("mm", ["T"], b - a, deps,
+                    lambda t, me: t.matmul_mx(T.ps[:, 512 * me["bank"]:512 * me["bank"] + b - a], w[:, k:k + 128], sw[:, k:k + 128],
+                                              q[:, a:b], s[:, a:b], True, True), at=at)
 
-    def transfer(d, codes, mask):
-        rid, pid = topo.addr(cores[d], core)
-        if codes:
-            src, dst = T.qw2[:].bitcast(dt.uint8), T["qr%d" % rank][:].bitcast(dt.uint8)
-        else:
-            src, dst = T.sw2[:], T["sr%d" % rank][:]
-        sent[0] += mask.bit_count()
-        return RemoteDMATransfer(src=src, dst=dst, dst_ids=[DstId(rid=rid, pnc=pid)], dma_engine_mask=mask, remote_sem=arr)
-
-    g.wait_ge(S.qw2, 2)
-    for k, d in enumerate(out):
-        for codes in (True, False):
-            ts = [transfer(d, codes, far)]
-            if k == 0:
-                ts += [transfer(o, codes, topo.mask(core, cores[o]) & ~far) for o in on]
-            g.remote_dma_fused(ts, local_sem=S.sent)
-
-    vec.wait_ge(S.lw1, 16)
-    vec.quantize_mx(T.qw1[:], T.sw1[:], T.w1t[:]).then_inc(S.qw1, 1)
-    bank = [0]
-    free = {}
-    waited = {}
-
-    def twait(name, n):
-        if waited.get(name, 0) < n:
-            ten.wait_ge(S[name], n)
-            waited[name] = n
-
-    def take():
-        b = bank[0] % 8
-        bank[0] += 1
-        if b in free:
-            twait(*free[b])
-        return b
-
-    def pair(w, sw, q, s, a, b, done):
-        bs = []
-        for i in range(2):
-            k = take()
-            ten.matmul_mx(T.ps[:, 512 * k:512 * k + b - a], w[:, 128 * i:128 * i + 128], sw[:, 128 * i:128 * i + 128],
-                          q[:, a:b], s[:, a:b], True, True).then_inc(S[done[i]], 1)
-            bs.append(k)
-        return bs
-
-    def acts(t, bs, skip, a, b, c, done, ev):
-        for i, q in ((0, act), (1, vec)):
-            q.wait_ge(S[done[i]], 1)
-            src = T.ps[:, 512 * bs[i] + skip:512 * bs[i] + skip + b - a]
-            for n, sign in ((0, 1.0), (1, -1.0)):
-                dst = t[:, 4 * a + 2 * i + n:4 * b:4]
-                if i == 0:
-                    act.activation(dst, src, relu, scale=sign * c).then_inc(S[ev], 1)
+    def leave(tile, i, mm, skip, a, b, c):
+        def emit(q, me):
+            k = 512 * tasks[mm]["bank"] + skip
+            for r, c2 in ((2 * i, c), (2 * i + 1, -c)):
+                dst, src = tile[:, 4 * a + r:4 * b:4], T.ps[:, k:k + b - a]
+                if me["q"] == "S":
+                    last = q.activation(dst, src, relu, scale=c2)
                 else:
-                    vec.tensor_scalar(dst, src, sign * c, 0.0, AluOpType.mult, AluOpType.max).then_inc(S[ev], 1)
+                    last = q.tensor_scalar(dst, src, c2, 0.0, AluOpType.mult, AluOpType.max)
+                if r == 2 * i:
+                    me["first"](last)
+            return last
+        return task("act", ["S", "V"], b - a, [mm], emit, calls=2)
 
-    def quant_x(c):
-        a, b = XCH[c]
-        vec.wait_ge(S["lx%d" % c], 16)
-        vec.quantize_mx(T.qx[:, a:b], T.sx[:, a:b], T.xt[:, 4 * a:4 * b]).then_inc(S["qx%d" % c], 1)
-
-    quant_x(0)
-    for c, (a, b) in enumerate(XCH):
-        done = ("za%d" % c, "zb%d" % c)
-        twait("qw1", 1)
-        twait("qx%d" % c, 1)
-        bs = pair(T.qw1, T.sw1, T.qx, T.sx, a, b, done)
-        for k in bs:
-            free[k] = ("qh%d" % c, 1)
-        acts(T.ht, bs, 0, a, b, C1, done, "ha%d" % c)
-        if c + 1 < len(XCH):
-            quant_x(c + 1)
-        vec.wait_ge(S["ha%d" % c], 4)
-        vec.quantize_mx(T.qh[:, a:b], T.sh[:, a:b], T.ht[:, 4 * a:4 * b]).then_inc(S["qh%d" % c], 1)
-    vec.wait_ge(S.lw3, 16)
-    vec.quantize_mx(T.qw3[:], T.sw3[:], T.w3t[:]).then_inc(S.qw3, 1)
-
-    pending, leaving, nun = [], [], [0]
-
-    def product():
-        for u, a, b in pending:
-            twait("qw3", 1)
-            twait("qg%d" % u, 1)
-            k = take()
-            free[k] = ("yc%d" % u, 1)
-            ten.matmul_mx(T.ps[:, 512 * k:512 * k + b - a], T.qw3[:], T.sw3[:], T.qg[:, a:b], T.sg[:, a:b],
-                          True, True).then_inc(S["yo%d" % u], 1)
-            leaving.append((u, a, b, k))
-        pending.clear()
-
-    def leave():
-        for u, a, b, k in leaving:
-            src = T.ps[:, 512 * k:512 * k + b - a]
-            if u % 2 == 0:
-                act.wait_ge(S["yo%d" % u], 1)
-                act.activation(T.ysb[:, a:b], src, copy).then_inc(S["yc%d" % u], 1)
-            else:
-                vec.wait_ge(S["yo%d" % u], 1)
-                vec.tensor_copy(T.ysb[:, a:b], src).then_inc(S["yc%d" % u], 1)
-            sync.wait_ge(S["yc%d" % u], 1)
-            sync.dma_start(T.y[:, a:b], T.ysb[:, a:b]).then_inc(S["st%d" % u], 16)
-        leaving.clear()
-
-    seen = []
-    for s, (e, a, b, late) in enumerate(steps):
-        if late:
-            product()
-            leave()
+    qw2 = [quant(T.qw2, T.sw2, T.w2t, 128 * i, 128 * i + 128, [], "w2" + "ab"[i]) for i in range(2)]
+    qw1 = quant(T.qw1, T.sw1, T.w1t, 0, WC, [], "w1")
+    qh = []
+    for c, (a, b) in enumerate(xch):
+        qx = quant(T.qx, T.sx, T.xt, a, b, [], "x%d" % c)
+        ms = [product(T.qw1, T.sw1, 128 * i, T.qx, T.sx, a, b, [qw1, qx]) for i in range(2)]
+        ls = [leave(T.ht, i, ms[i], 0, a, b, C1) for i in range(2)]
+        qh.append(quant(T.qh, T.sh, T.ht, a, b, ls))
+    qw3 = quant(T.qw3, T.sw3, T.w3t, 0, 128, [], "w3")
+    ga = []
+    for e, a, b, place in steps:
         lo, hi = a, b
         if hi - lo < MIN:
             lo = min(lo, NC - MIN)
             hi = lo + MIN
-        for c, (p, q) in enumerate(XCH):
-            if p < hi and lo < q:
-                twait("qh%d" % c, 1)
+        deps = [qh[c] for c, (p, q) in enumerate(xch) if p < hi and lo < q]
         if e == rank:
-            twait("qw2", 2)
-            w, sw = T.qw2, T.sw2
+            w, sw, at = T.qw2, T.sw2, 0.0
+            deps = deps + qw2
         else:
-            son, sout = sends(cnt, cores, e, topo)
-            ofar = topo.mask(cores[e], cores[sout[0]])
-            m = ofar if rank in sout else topo.mask(cores[e], core) & ~ofar
-            twait("arr%d" % e, 2 * m.bit_count())
-            w, sw = T["qr%d" % e], T["sr%d" % e]
-        done, ev = ("ya%d" % s, "yb%d" % s), "ga%d" % s
-        bs = pair(w, sw, T.qh, T.sh, lo, hi, done)
-        for k in bs:
-            free[k] = (ev, 4)
-        product()
-        acts(T.gt, bs, a - lo, a, b, C2, done, ev)
-        seen.append((a, b, ev))
-        fresh = []
-        for p, q in units[s]:
-            for a2, b2, ev2 in seen:
-                if a2 < q and p < b2:
-                    vec.wait_ge(S[ev2], 4)
-            u = nun[0]
-            nun[0] += 1
-            vec.quantize_mx(T.qg[:, p:q], T.sg[:, p:q], T.gt[:, 4 * p:4 * q]).then_inc(S["qg%d" % u], 1)
-            fresh.append((u, p, q))
-        leave()
-        pending.extend(fresh)
-    product()
-    leave()
-    for u in range(nun[0]):
-        sync.wait_ge(S["st%d" % u], 16)
+            w, sw, at = T["qr%d" % e], T["sr%d" % e], ARRIVE[place] + WAKE
+        ms = [product(w, sw, 128 * i, T.qh, T.sh, lo, hi, deps, at) for i in range(2)]
+        if e != rank:
+            come.update({m: e for m in ms})
+        ga.append([leave(T.gt, i, ms[i], a - lo, a, b, C2) for i in range(2)])
+    stores = []
+    for a, b in units:
+        deps = [t for (_, p, q, _k), ts in zip(steps, ga) if p < b and a < q for t in ts]
+        qg = quant(T.qg, T.sg, T.gt, a, b, deps)
+        m = product(T.qw3, T.sw3, 0, T.qg, T.sg, a, b, [qw3, qg])
+
+        def out(q, me, a=a, b=b, m=m):
+            src = T.ps[:, 512 * tasks[m]["bank"]:512 * tasks[m]["bank"] + b - a]
+            return q.activation(T.ysb[:, a:b], src, copy) if me["q"] == "S" else q.tensor_copy(T.ysb[:, a:b], src)
+        o = task("act", ["S", "V"], b - a, [m], out)
+        stores.append(task("store", ["sync"], b - a, [o], lambda q, me, a=a, b=b: q.dma_start(T.y[:, a:b], T.ysb[:, a:b])))
+    order = schedule(tasks)
+
+    held = {q: set() for q in queues}
+    for i in order:
+        t = tasks[i]
+        t["waits"] = []
+        k = held[t["q"]]
+        for d in sorted(t["deps"], reverse=True, key=lambda d: tasks[d]["start"]):
+            if d not in k:
+                t["waits"].append(d)
+                k |= tasks[d]["known"] | {d}
+        t["known"] = set(k)
+    waited = set(d for t in tasks for d in t["waits"]) | set(stores) | set(qw2)
+
+    def fetch(q, name, tile, src, a, b):
+        queues[q].dma_start(tile[:, a:b], src[:, a:b]).then_inc(S["l" + name], 16)
+    (a0, b0), (a1, b1) = xch
+    fetch("sync", "w2a", T.w2t, T.w2, 0, 512)
+    fetch("S", "w2b", T.w2t, T.w2, 512, 1024)
+    fetch("sync", "w1", T.w1t, T.w1, 0, 1024)
+    fetch("S", "x0", T.xt, T.x, 4 * a0, 4 * b0)
+    fetch("sync", "x1", T.xt, T.x, 4 * a1, 4 * b1)
+    fetch("sync", "w3", T.w3t, T.w3, 0, 512)
+
+    sent = [0]
+
+    def transfer(e, d, codes):
+        q, s = (T.qw2, T.sw2) if e == rank else (T["qr%d" % e], T["sr%d" % e])
+        if codes:
+            src, dst = q[:].bitcast(dt.uint8), T["qr%d" % e][:].bitcast(dt.uint8)
+        else:
+            src, dst = s[:], T["sr%d" % e][:]
+        rid, pid = topo.addr(cores[d], core)
+        mask = engines(cnt, cores, e, d, topo)
+        sent[0] += mask.bit_count()
+        return RemoteDMATransfer(src=src, dst=dst, dst_ids=[DstId(rid=rid, pnc=pid)], dma_engine_mask=mask,
+                                 remote_sem=S[("codes%d" if codes else "plane%d") % e])
+
+    on, outs = sends(cnt, cores, rank, topo)
+    for d in qw2:
+        g.wait_ge(S["t%d" % d], 1)
+    for codes in (True, False):
+        g.remote_dma_fused([transfer(rank, d, codes) for d in outs[:1] + on], local_sem=S.sent)
+    for e in range(len(cores)):
+        eout = sends(cnt, cores, e, topo)[1]
+        if e != rank and len(eout) > 1 and eout[0] == rank:
+            n = engines(cnt, cores, e, rank, topo).bit_count()
+            for codes in (True, False):
+                g.wait_ge(S[("codes%d" if codes else "plane%d") % e], n)
+                g.remote_dma_fused([transfer(e, d, codes) for d in eout[1:]], local_sem=S.sent)
+
+    def parts(i):
+        return 16 if tasks[i]["kind"] == "store" else tasks[i]["calls"]
+    arrived = set()
+    for i in order:
+        t = tasks[i]
+        q = queues[t["q"]]
+        if i in load:
+            q.wait_ge(S["l" + load[i]], 16)
+        if i in come and come[i] not in arrived:
+            e = come[i]
+            arrived.add(e)
+            n = engines(cnt, cores, e, rank, topo).bit_count()
+            q.wait_ge(S["codes%d" % e], n)
+            q.wait_ge(S["plane%d" % e], n)
+        for d in t["waits"]:
+            q.wait_ge(S["t%d" % d], parts(d))
+        if i in waited:
+            t["first"] = lambda ins, i=i: ins.then_inc(S["t%d" % i], 1)
+            t["emit"](q, t).then_inc(S["t%d" % i], 16 if t["kind"] == "store" else 1)
+        else:
+            t["first"] = lambda ins: None
+            t["emit"](q, t)
+    for i in stores:
+        g.sync.wait_ge(S["t%d" % i], 16)
     g.wait_ge(S.sent, sent[0])

import numpy as np
from concourse.bass import DstId, RemoteDMATransfer
from concourse.mybir import dt, AluOpType, ActivationFunctionType

NC = 512
MIN = 128
WC = 256
RANKS = 4
CUT = 256
C1, C2 = float(np.float32(0.031)), float(np.float32(0.023))
BANKS = 8
WAKE = 0.14
SLACK = 0.04
LOADED = {"w2a": 1.3, "w2b": 1.7, "w1": 2.8, "x0": 2.3, "x1": 3.7, "w3": 3.9}
ARRIVE = [5.5, 5.5, 7.0]
COST = {"quant": (0.03, 0.0009), "mm": (0.04, 0.0008), "S": (0.10, 0.00083), "V": (0.03, 0.00083), "store": (0.08, 0.0)}

SCRATCH = {
    "xt": ("sbuf", [128, 4 * NC], "bfloat16"), "w1t": ("sbuf", [128, 1024], "bfloat16"),
    "w2t": ("sbuf", [128, 1024], "bfloat16"), "w3t": ("sbuf", [128, 512], "bfloat16"),
    "ht": ("sbuf", [128, 4 * NC], "bfloat16"), "gt": ("sbuf", [128, 4 * NC], "bfloat16"),
    "ysb": ("sbuf", [128, NC], "float32"),
    "ps": ("psum", [128, 512 * BANKS], "float32"),
}
for _n, _w in [("x", NC), ("w1", WC), ("w2", WC), ("w3", 128), ("h", NC), ("g", NC)] + [("r%d" % _e, WC) for _e in range(RANKS)]:
    SCRATCH["q" + _n] = ("sbuf", [128, _w], "float8_e4m3fn_x4")
    SCRATCH["s" + _n] = ("sbuf", [128, _w], "uint8")

NTASK = 90
SEMAPHORES = ["l" + n for n in LOADED] + ["%s%d" % (n, e) for e in range(RANKS) for n in ("codes", "plane")]
SEMAPHORES += ["t%d" % i for i in range(NTASK)] + ["sent"]


def here(a, b, topo):
    return topo.host(a) == topo.host(b) and topo.chip(a) == topo.chip(b)


def sends(cnt, cores, rank, topo):
    need = sorted((d for d in range(len(cores)) if d != rank and cnt[d][rank]), key=lambda d: -cnt[d][rank])
    return [d for d in need if here(cores[d], cores[rank], topo)], [d for d in need if not here(cores[d], cores[rank], topo)]


def engines(cnt, cores, e, d, topo):
    out = sends(cnt, cores, e, topo)[1]
    far = topo.mask(cores[e], cores[out[0]])
    if d == out[0]:
        return far
    if d in out:
        return topo.mask(cores[out[0]], cores[d])
    return topo.mask(cores[e], cores[d]) & ~far


def plan(cnt, cores, rank, topo):
    off = [sum(cnt[rank][:e]) for e in range(len(cores) + 1)]
    segs = []
    for e in range(len(cores)):
        if not cnt[rank][e]:
            continue
        if e == rank:
            key = -1
        else:
            on, out = sends(cnt, cores, e, topo)
            key = 0 if rank in on else 1 + out.index(rank)
        segs.append((key, e, off[e], off[e + 1]))
    steps = []
    for key, e, a, b in sorted(segs):
        m = a + (b - a) // 4 * 2 if b - a > CUT else b
        for p, q in [(a, m), (m, b)]:
            if q > p:
                steps.append((e, p, q, key))
    state = [0] * NC
    units = []
    for _, a, b, _k in steps:
        state[a:b] = [1] * (b - a)
        i = 0
        while i < NC:
            j = i
            while j < NC and state[j] == state[i]:
                j += 1
            if state[i] == 1:
                lo, hi, k = i, j, i
                while k > 0 and state[k - 1] == 0:
                    k -= 1
                if 0 < lo - k < MIN:
                    lo += MIN - (lo - k)
                k = hi
                while k < NC and state[k] == 0:
                    k += 1
                if 0 < k - hi < MIN:
                    hi -= MIN - (k - hi)
                if hi - lo >= MIN:
                    state[lo:hi] = [2] * (hi - lo)
                    units.append((lo, hi))
            i = j
    return steps, units


def halves(units):
    lo, hi = units[0]
    for a, b in units[1:]:
        if hi - lo >= NC // 2 - 40 or (a != hi and b != lo):
            break
        lo, hi = min(lo, a), max(hi, b)
    if lo == 0:
        return [(0, hi), (hi, NC)]
    return [(lo, NC), (0, lo)]


def schedule(tasks):
    users = [[] for _ in tasks]
    for i, t in enumerate(tasks):
        for d in t["deps"]:
            users[d].append(i)

    def dur(t, q):
        c = COST[q] if t["kind"] == "act" else COST[t["kind"]]
        return t["calls"] * (c[0] + c[1] * t["n"])
    way = [0.0] * len(tasks)
    for i in reversed(range(len(tasks))):
        way[i] = max(dur(tasks[i], q) for q in tasks[i]["eng"]) + max([way[u] + WAKE for u in users[i]] + [0.0])
    free = {}
    banks = [(0.0, [])] * BANKS
    holds = {}
    order, left = [], set(range(len(tasks)))
    while left:
        cands = []
        for i in sorted(left):
            t = tasks[i]
            if any(d in left for d in t["deps"]):
                continue
            at = max([t["at"]] + [tasks[d]["end"] + WAKE for d in t["deps"]])
            bank = None
            if t["kind"] == "mm":
                ready = [(max(at, banks[k][0]), k) for k in range(BANKS) if banks[k] is not None]
                if not ready:
                    continue
                at, bank = min(ready)
            starts = [(max(at, free.get(q, 0.0)), q) for q in t["eng"]]
            _, start, q = min((x + dur(t, q), x, q) for x, q in starts)
            cands.append((start, -way[i], i, q, bank))
        first = min(cands)
        start, _, i, q, bank = min((c for c in cands if c[3] == first[3] and c[0] <= first[0] + SLACK), key=lambda c: c[1:4])
        t = tasks[i]
        left.remove(i)
        order.append(i)
        t["q"], t["start"], t["end"] = q, start, start + dur(t, q)
        free[q] = t["end"]
        if bank is not None:
            t["deps"] = t["deps"] + banks[bank][1]
            t["bank"] = bank
            banks[bank] = None
            holds[i] = bank
        for d in t["deps"]:
            if d in holds and t["kind"] == "act":
                banks[holds[d]] = (t["end"] + WAKE, [i])
                del holds[d]
    return order


def rank_program(g, core, T, topo):
    rank = T.rank_of(core)
    if rank is None:
        return
    cnt, cores, S = T.tables["CNT"], T.cores, T.sem
    steps, units = plan(cnt, cores, rank, topo)
    xch = halves(units)
    queues = {"S": g.scalar, "V": g.vector, "T": g.tensor, "sync": g.sync}
    relu, copy = ActivationFunctionType.Relu, ActivationFunctionType.Copy
    tasks = []
    load = {}
    come = {}

    def task(kind, eng, n, deps, emit, calls=1, at=0.0):
        tasks.append(dict(kind=kind, eng=eng, n=n, deps=deps, emit=emit, calls=calls, at=at))
        return len(tasks) - 1

    def quant(q, s, t, a, b, deps, name=None):
        i = task("quant", ["V"], b - a, deps,
                 lambda v, me: v.quantize_mx(q[:, a:b], s[:, a:b], t[:, 4 * a:4 * b]), at=LOADED[name] + WAKE if name else 0.0)
        if name:
            load[i] = name
        return i

    def product(w, sw, k, q, s, a, b, deps, at=0.0):
        return task("mm", ["T"], b - a, deps,
                    lambda t, me: t.matmul_mx(T.ps[:, 512 * me["bank"]:512 * me["bank"] + b - a], w[:, k:k + 128], sw[:, k:k + 128],
                                              q[:, a:b], s[:, a:b], True, True), at=at)

    def leave(tile, i, mm, skip, a, b, c):
        def emit(q, me):
            k = 512 * tasks[mm]["bank"] + skip
            for r, c2 in ((2 * i, c), (2 * i + 1, -c)):
                dst, src = tile[:, 4 * a + r:4 * b:4], T.ps[:, k:k + b - a]
                if me["q"] == "S":
                    last = q.activation(dst, src, relu, scale=c2)
                else:
                    last = q.tensor_scalar(dst, src, c2, 0.0, AluOpType.mult, AluOpType.max)
                if r == 2 * i:
                    me["first"](last)
            return last
        return task("act", ["S", "V"], b - a, [mm], emit, calls=2)

    qw2 = [quant(T.qw2, T.sw2, T.w2t, 128 * i, 128 * i + 128, [], "w2" + "ab"[i]) for i in range(2)]
    qw1 = quant(T.qw1, T.sw1, T.w1t, 0, WC, [], "w1")
    qh = []
    for c, (a, b) in enumerate(xch):
        qx = quant(T.qx, T.sx, T.xt, a, b, [], "x%d" % c)
        ms = [product(T.qw1, T.sw1, 128 * i, T.qx, T.sx, a, b, [qw1, qx]) for i in range(2)]
        ls = [leave(T.ht, i, ms[i], 0, a, b, C1) for i in range(2)]
        qh.append(quant(T.qh, T.sh, T.ht, a, b, ls))
    qw3 = quant(T.qw3, T.sw3, T.w3t, 0, 128, [], "w3")
    ga = []
    for e, a, b, place in steps:
        lo, hi = a, b
        if hi - lo < MIN:
            lo = min(lo, NC - MIN)
            hi = lo + MIN
        deps = [qh[c] for c, (p, q) in enumerate(xch) if p < hi and lo < q]
        if e == rank:
            w, sw, at = T.qw2, T.sw2, 0.0
            deps = deps + qw2
        else:
            w, sw, at = T["qr%d" % e], T["sr%d" % e], ARRIVE[place] + WAKE
        ms = [product(w, sw, 128 * i, T.qh, T.sh, lo, hi, deps, at) for i in range(2)]
        if e != rank:
            come.update({m: e for m in ms})
        ga.append([leave(T.gt, i, ms[i], a - lo, a, b, C2) for i in range(2)])
    stores = []
    for a, b in units:
        deps = [t for (_, p, q, _k), ts in zip(steps, ga) if p < b and a < q for t in ts]
        qg = quant(T.qg, T.sg, T.gt, a, b, deps)
        m = product(T.qw3, T.sw3, 0, T.qg, T.sg, a, b, [qw3, qg])

        def out(q, me, a=a, b=b, m=m):
            src = T.ps[:, 512 * tasks[m]["bank"]:512 * tasks[m]["bank"] + b - a]
            return q.activation(T.ysb[:, a:b], src, copy) if me["q"] == "S" else q.tensor_copy(T.ysb[:, a:b], src)
        o = task("act", ["S", "V"], b - a, [m], out)
        stores.append(task("store", ["sync"], b - a, [o], lambda q, me, a=a, b=b: q.dma_start(T.y[:, a:b], T.ysb[:, a:b])))
    order = schedule(tasks)

    held = {q: set() for q in queues}
    for i in order:
        t = tasks[i]
        t["waits"] = []
        k = held[t["q"]]
        for d in sorted(t["deps"], reverse=True, key=lambda d: tasks[d]["start"]):
            if d not in k:
                t["waits"].append(d)
                k |= tasks[d]["known"] | {d}
        t["known"] = set(k)
    waited = set(d for t in tasks for d in t["waits"]) | set(stores) | set(qw2)

    def fetch(q, name, tile, src, a, b):
        queues[q].dma_start(tile[:, a:b], src[:, a:b]).then_inc(S["l" + name], 16)
    (a0, b0), (a1, b1) = xch
    fetch("sync", "w2a", T.w2t, T.w2, 0, 512)
    fetch("S", "w2b", T.w2t, T.w2, 512, 1024)
    fetch("sync", "w1", T.w1t, T.w1, 0, 1024)
    fetch("S", "x0", T.xt, T.x, 4 * a0, 4 * b0)
    fetch("sync", "x1", T.xt, T.x, 4 * a1, 4 * b1)
    fetch("sync", "w3", T.w3t, T.w3, 0, 512)

    sent = [0]

    def transfer(e, d, codes):
        q, s = (T.qw2, T.sw2) if e == rank else (T["qr%d" % e], T["sr%d" % e])
        if codes:
            src, dst = q[:].bitcast(dt.uint8), T["qr%d" % e][:].bitcast(dt.uint8)
        else:
            src, dst = s[:], T["sr%d" % e][:]
        rid, pid = topo.addr(cores[d], core)
        mask = engines(cnt, cores, e, d, topo)
        sent[0] += mask.bit_count()
        return RemoteDMATransfer(src=src, dst=dst, dst_ids=[DstId(rid=rid, pnc=pid)], dma_engine_mask=mask,
                                 remote_sem=S[("codes%d" if codes else "plane%d") % e])

    on, outs = sends(cnt, cores, rank, topo)
    for d in qw2:
        g.wait_ge(S["t%d" % d], 1)
    for codes in (True, False):
        g.remote_dma_fused([transfer(rank, d, codes) for d in outs[:1] + on], local_sem=S.sent)
    for e in range(len(cores)):
        eout = sends(cnt, cores, e, topo)[1]
        if e != rank and len(eout) > 1 and eout[0] == rank:
            n = engines(cnt, cores, e, rank, topo).bit_count()
            for codes in (True, False):
                g.wait_ge(S[("codes%d" if codes else "plane%d") % e], n)
                g.remote_dma_fused([transfer(e, d, codes) for d in eout[1:]], local_sem=S.sent)

    def parts(i):
        return 16 if tasks[i]["kind"] == "store" else tasks[i]["calls"]
    arrived = set()
    for i in order:
        t = tasks[i]
        q = queues[t["q"]]
        if i in load:
            q.wait_ge(S["l" + load[i]], 16)
        if i in come and come[i] not in arrived:
            e = come[i]
            arrived.add(e)
            n = engines(cnt, cores, e, rank, topo).bit_count()
            q.wait_ge(S["codes%d" % e], n)
            q.wait_ge(S["plane%d" % e], n)
        for d in t["waits"]:
            q.wait_ge(S["t%d" % d], parts(d))
        if i in waited:
            t["first"] = lambda ins, i=i: ins.then_inc(S["t%d" % i], 1)
            t["emit"](q, t).then_inc(S["t%d" % i], 16 if t["kind"] == "store" else 1)
        else:
            t["first"] = lambda ins: None
            t["emit"](q, t)
    for i in stores:
        g.sync.wait_ge(S["t%d" % i], 16)
    g.wait_ge(S.sent, sent[0])
